import numpy as np
import ml_dtypes


def mxq(x, axis, fmt="e4m3"):
    dtype, down = {"e4m3": (ml_dtypes.float8_e4m3fn, 7), "e5m2": (ml_dtypes.float8_e5m2, 14)}[fmt]
    v = np.moveaxis(np.asarray(x, np.float32).astype(ml_dtypes.bfloat16).astype(np.float64), axis, -1)
    blocks = v.reshape(v.shape[:-1] + (-1, 32))
    amax = np.abs(blocks).max(-1, keepdims=True)
    byte = np.maximum(np.where(amax > 0, np.frexp(amax)[1] - 1 + 127, 0) - down, 1)
    scale = np.exp2(byte - 127.0)
    codes = (blocks / scale).astype(np.float32).astype(dtype).astype(np.float64)
    return np.moveaxis((codes * scale).reshape(v.shape), -1, axis)


WIDE = False


def mx_kscale(k):
    if not WIDE:
        return np.ones(k)
    levels = np.array([10, -10, 5, -5, 0])
    if k % 512:
        return np.exp2(np.random.permutation(np.resize(levels, k // 32))).repeat(32)
    a = np.empty((k // 512, 16))
    for p in range(k // 512):
        a[p, :8] = np.random.permutation(np.resize(levels, 8))
        for g in range(8):
            far = levels[np.abs(levels - a[p, g]) >= 10]
            a[p, g + 8] = far[np.random.randint(len(far))]
    return np.exp2(a.ravel()).repeat(32)


def f64(x):
    return np.asarray(x).astype(np.float64)


def striped(idx):
    return np.tile(idx.reshape(-1, 16).T, (8, 1)).astype(np.uint16)


def unstriped(offs):
    return offs[:16].T.reshape(-1).astype(np.int64)


def striped8(idx):
    return np.concatenate([x.reshape(-1, 16).T for x in idx]).astype(np.uint16)


def runs(offs, k):
    lists = np.stack([offs[16 * r : 16 * r + 16].T.reshape(-1) for r in range(8)]).astype(np.int64)
    return lists[np.arange(k) % 512 // 64]


def pack_weight(w):
    k, n = w.shape
    w = f64(np.asarray(w, np.float32).astype(ml_dtypes.bfloat16)).reshape(k // 32, 32, n)
    amax = np.abs(w).max(1)
    byte = np.clip(np.where(amax > 0, np.frexp(amax)[1] - 1 + 127 - 7, 1), 1, 254)
    scaled = (w * np.exp2(127.0 - byte)[:, None, :]).reshape(k, n).astype(np.float32)
    words = np.ascontiguousarray(scaled.reshape(k // 512, 128, 4, n).transpose(0, 1, 3, 2)).astype(ml_dtypes.float8_e4m3fn).view(np.uint8)
    return words, np.ascontiguousarray(byte.astype(np.uint8).reshape(k // 512, 16, n))


def unpack_weight(words, scales):
    g, p, n, _ = words.shape
    vals = np.ascontiguousarray(words).view(ml_dtypes.float8_e4m3fn).astype(np.float64) * np.repeat(np.exp2(scales.astype(np.float64) - 127.0), 8, axis=1)[..., None]
    return vals.transpose(0, 1, 3, 2).reshape(g * 512, n)

def planes(y):
    n, m = y.shape
    v = y.astype(np.float32).astype(ml_dtypes.bfloat16).astype(np.float64).reshape(n // 32, 32, m)
    top = np.abs(v).max(1)
    byte = np.clip(np.where(top > 0, np.frexp(top)[1] - 1 + 127 - 7, 1), 1, 254)
    codes = (v * np.exp2(127.0 - byte)[:, None, :]).reshape(n, m).astype(np.float32).astype(ml_dtypes.float8_e4m3fn).view(np.uint8)
    words = codes.reshape(n // 512, 128, 4, m).transpose(0, 1, 3, 2)
    return np.ascontiguousarray(words), np.ascontiguousarray(byte.astype(np.uint8).reshape(n // 512, 16, m))


K, T, S, N, H, W = 512, 2048, 512, 512, 512, 256


def setup_inputs():
    n = np.random.standard_normal
    s = mx_kscale(K)[:, None]
    u = mx_kscale(H)
    packed_xT = pack_weight(n((K, T)) * s)
    packed_w1 = pack_weight(n((K, H)) / np.sqrt(K) / s)
    packed_w2 = pack_weight(n((H, N)) / np.sqrt(H) / u[:, None])
    return {
        "x_words": packed_xT[0],
        "x_scales": packed_xT[1],
        "w1_words": packed_w1[0],
        "w1_scales": packed_w1[1],
        "gn": (np.random.uniform(0.5, 1.5, (H, 1)) * u[:, None]).astype(np.float32),
        "w2_words": packed_w2[0],
        "w2_scales": packed_w2[1],
        "offs": striped(np.random.permutation(T)[:S]),
        "n1": striped8(np.stack([np.random.permutation(S) for _ in range(8)])),
        "n2": striped8(np.stack([np.random.permutation(S) for _ in range(8)])),
        "n3": striped8(np.stack([np.random.permutation(S)[:W] for _ in range(8)])),
        "n4": striped8(np.stack([np.random.permutation(S)[:W] for _ in range(8)])),
    }


def reference(x_words, x_scales, w1_words, w1_scales, gn, w2_words, w2_scales, offs, n1, n2, n3, n4):
    xq = unpack_weight(x_words, x_scales)[:, unstriped(offs)]
    y = unpack_weight(w1_words, w1_scales).T @ xq
    st = y + 0.5 * (y[np.arange(H)[:, None], runs(n1, H)])
    z = f64(gn) * (st - (st[np.arange(H)[:, None], runs(n2, H)]))
    h = unpack_weight(w2_words, w2_scales).T @ mxq(z, 0, "e4m3")
    ra = y[np.arange(H)[:, None], runs(n4, H)] - (0.5 * (h[np.arange(N)[:, None], runs(n3, N)]))
    out = h.copy()
    out[np.arange(H)[:, None], runs(n3, H)] = ra
    return (out,) + planes(out)

@@ -1,0 +1,198 @@
+from contextlib import ExitStack
+
+import concourse.mybir as mybir
+
+K, T, S, N, H, W = 512, 2048, 512, 512, 512, 256
+FLOPS = 2 * K * H * S + 2 * H * N * S
+
+F32 = mybir.dt.float32
+BF16 = mybir.dt.bfloat16
+I32 = mybir.dt.int32
+U32 = mybir.dt.uint32
+U16 = mybir.dt.uint16
+U8 = mybir.dt.uint8
+FP8X4 = mybir.dt.float8_e4m3fn_x4
+ADD = mybir.AluOpType.add
+SUB = mybir.AluOpType.subtract
+MULT = mybir.AluOpType.mult
+COPY = mybir.ActivationFunctionType.Copy
+
+P = 128
+PACK = 4
+HALF = S // 2
+Z_CHUNKS = ((0, 256), (256, 128), (384, 128))
+
+
+def tile_picked_skipputbhop_none_po_kernel(tc, x_words, x_scales, w1_words, w1_scales, gn, w2_words, w2_scales, offs, n1, n2, n3, n4, out_0, out_1, out_2):
+    nc = tc.nc
+    with ExitStack() as ctx:
+        keep = ctx.enter_context(tc.tile_pool(name="keep", bufs=1))
+        psum = ctx.enter_context(tc.psum_pool(name="psum", bufs=1))
+
+        def sb(name, shape, dtype):
+            return keep.tile(shape, dtype, name=name, align_bytes=64)
+
+        def load_list(name, src):
+            tile = keep.tile(list(src.shape), U16, name=name)
+            nc.sync.dma_start(tile[:], src)
+            return tile
+
+        def cols16(lst, start, count):
+            return lst[:, start // 16 : (start + count) // 16]
+
+        def load_scales(queue, tile, src):
+            for q in range(4):
+                queue.dma_start(tile[32 * q : 32 * q + 4, :].bitcast(I32), src[0, 4 * q : 4 * q + 4, :].bitcast(I32))
+
+        def load_words(tile, src):
+            nc.sync.dma_start(tile[:], src[0].rearrange("p c r -> p (c r)").bitcast(I32))
+
+        xs = sb("xs", [P, T], U8)
+        w1s_raw = sb("w1s_raw", [P, H], U8)
+        w2s_raw = sb("w2s_raw", [P, N], U8)
+        warm = sb("warm", [P, 2], F32)
+        nc.vector.memset(xs[:].bitcast(I32), 0)
+        nc.vector.memset(w1s_raw[:].bitcast(I32), 0)
+        nc.vector.memset(w2s_raw[:].bitcast(I32), 0)
+        nc.vector.memset(warm[:, 0:1], 0.0)
+
+        load_scales(nc.scalar, xs, x_scales)
+        nc.scalar.activation(warm[:, 1:2], warm[:, 0:1], COPY, scale=-1.0)
+        xw = sb("xw", [P, T], I32)
+        load_words(xw, x_words)
+        offs_t = load_list("offs_t", offs)
+        w1w_raw = sb("w1w_raw", [P, H], I32)
+        load_words(w1w_raw, w1_words)
+        load_scales(nc.sync, w1s_raw, w1_scales)
+        gain = sb("gain", [P, PACK], F32)
+        nc.sync.dma_start(gain[:], gn.rearrange("(p t) o -> p (t o)", t=PACK))
+        n1_t = load_list("n1_t", n1)
+        w2w_raw = sb("w2w_raw", [P, N], I32)
+        load_words(w2w_raw, w2_words)
+        load_scales(nc.sync, w2s_raw, w2_scales)
+        n2_t = load_list("n2_t", n2)
+        n4_t = load_list("n4_t", n4)
+        n3_t = load_list("n3_t", n3)
+
+        def deal(name, raw, dtype):
+            tile = sb(name, [P, PACK, P], dtype)
+            nc.vector.tensor_copy(tile[:], raw[:].rearrange("p (m t) -> p t m", t=PACK))
+            return tile
+
+        xg_s = sb("xg_s", [P, S], U8)
+        nc.vector.tensor_copy(xg_s[:], xs[:].indirect(offs_t[:]))
+        w1w = deal("w1w", w1w_raw, I32)
+        w1s = deal("w1s", w1s_raw, U8)
+
+        neg_gain = sb("neg_gain", [P, PACK], F32)
+        neg_half = sb("neg_half", [P, PACK], F32)
+        nc.scalar.activation(neg_gain[:], gain[:], COPY, scale=-1.0)
+        nc.scalar.activation(neg_half[:], gain[:], COPY, scale=-0.5)
+
+        y_ps = {}
+        for c in range(2):
+            xg_w = sb("xg_w%d" % c, [P, HALF], U32)
+            nc.vector.tensor_copy(xg_w[:], xw[:].bitcast(U32).indirect(cols16(offs_t, c * HALF, HALF)))
+            for u in range(2):
+                bank = psum.tile([P, 2, HALF], F32, name="y_ps%d%d" % (c, u))
+                for e in range(2):
+                    t = 2 * u + e
+                    nc.tensor.matmul_mx(
+                        out=bank[:, e, :],
+                        lhsT=w1w[:, t, :].bitcast(FP8X4),
+                        lhsT_scale=w1s[:, t, :],
+                        rhs=xg_w[:].bitcast(FP8X4),
+                        rhs_scale=xg_s[:, c * HALF : (c + 1) * HALF],
+                        start=True,
+                        stop=True,
+                    )
+                    y_ps[c, t] = bank[:, e, :]
+
+        w2w = deal("w2w", w2w_raw, I32)
+        w2s = deal("w2s", w2s_raw, U8)
+
+        halves = [slice(c * HALF, (c + 1) * HALF) for c in range(2)]
+        st = []
+        for t in range(PACK):
+            y_half = sb("y_half%d" % t, [P, S], F32)
+            y_full = sb("y_full%d" % t, [P, S], F32)
+            for c in range(2):
+                nc.scalar.activation(y_half[:, halves[c]], y_ps[c, t], COPY, scale=neg_half[:, t : t + 1])
+                nc.scalar.activation(y_full[:, halves[c]], y_ps[c, t], COPY, scale=neg_gain[:, t : t + 1])
+            s_t = sb("st%d" % t, [P, S], F32)
+            for c in range(2):
+                nc.vector.tensor_tensor(s_t[:, halves[c]], y_half[:].indirect(cols16(n1_t, c * HALF, HALF)), y_full[:, halves[c]], ADD)
+            st.append(s_t)
+
+        st_copy = []
+        for t in range(PACK):
+            cp = sb("st_copy%d" % t, [P, S], F32)
+            if t < 2:
+                nc.sync.dma_start(cp[:], st[t][:])
+            else:
+                nc.scalar.copy(cp[:], st[t][:])
+            st_copy.append(cp)
+
+        y_raw = []
+        for t in range(PACK):
+            y_t = sb("y_raw%d" % t, [P, S], F32)
+            for c in range(2):
+                nc.scalar.copy(y_t[:, halves[c]], y_ps[c, t])
+            y_raw.append(y_t)
+
+        h = [sb("h%d" % t, [P, S], F32) for t in range(PACK)]
+        for start, width in Z_CHUNKS:
+            cols = slice(start, start + width)
+            z = sb("z%d" % start, [P, PACK, width], F32)
+            for t in range(PACK):
+                nc.vector.tensor_tensor(z[:, t, :], st[t][:].indirect(cols16(n2_t, start, width)), st_copy[t][:, cols], SUB)
+            zb = sb("zb%d" % start, [P, width, PACK], BF16)
+            nc.scalar.copy(zb[:].rearrange("p (c i) t -> p c t i", i=4), z[:].rearrange("p t (c i) -> p c t i", i=4))
+            zw = sb("zw%d" % start, [P, width], U32)
+            zs = sb("zs%d" % start, [P, width], U8)
+            nc.vector.quantize_mx(out=zw[:].bitcast(FP8X4), scales=zs[:], in_=zb[:].rearrange("p c t -> p (c t)"))
+            per_bank = S // width
+            for u in range(PACK // per_bank):
+                bank = psum.tile([P, per_bank, width], F32, name="h_ps%d_%d" % (start, u))
+                for e in range(per_bank):
+                    t = per_bank * u + e
+                    nc.tensor.matmul_mx(
+                        out=bank[:, e, :],
+                        lhsT=w2w[:, t, :].bitcast(FP8X4),
+                        lhsT_scale=w2s[:, t, :],
+                        rhs=zw[:].bitcast(FP8X4),
+                        rhs_scale=zs[:],
+                        start=True,
+                        stop=True,
+                    )
+                for e in range(per_bank):
+                    nc.scalar.copy(h[per_bank * u + e][:, cols], bank[:, e, :])
+
+        y_n4 = []
+        for t in range(PACK):
+            g = sb("y_n4_%d" % t, [P, W], F32)
+            nc.vector.tensor_copy(g[:], y_raw[t][:].indirect(n4_t[:]))
+            y_n4.append(g)
+
+        out_rows = out_0.rearrange("(p t) j -> t p j", t=PACK)
+        ob = [sb("ob%d" % c, [P, HALF, PACK], BF16) for c in range(2)]
+        for t in range(PACK):
+            g = sb("h_n3_%d" % t, [P, W], F32)
+            nc.vector.tensor_scalar(g[:], h[t][:].indirect(n3_t[:]), -0.5, 0.0, MULT, ADD)
+            nc.vector.tensor_tensor(h[t][:].indirect(n3_t[:]), y_n4[t][:], g[:], ADD)
+            nc.sync.dma_start(out_rows[t], h[t][:])
+            if t < 2:
+                nc.scalar.copy(ob[0][:, :, t], h[t][:, halves[0]])
+            else:
+                nc.vector.tensor_copy(ob[0][:, :, t], h[t][:, halves[0]])
+            nc.scalar.copy(ob[1][:, :, t], h[t][:, halves[1]])
+
+        os_t = sb("os_t", [P, S], U8)
+        words_out = out_1[0].rearrange("p c r -> p (c r)").bitcast(I32)
+        for c in range(2):
+            ow = sb("ow%d" % c, [P, HALF], U32)
+            nc.vector.quantize_mx(out=ow[:].bitcast(FP8X4), scales=os_t[:, halves[c]], in_=ob[c][:].rearrange("p c t -> p (c t)"))
+            nc.sync.dma_start(words_out[:, halves[c]], ow[:].bitcast(I32))
+        for q in range(4):
+            queue = nc.sync if q % 2 == 0 else nc.scalar
+            queue.dma_start(out_2[0, 4 * q : 4 * q + 4, :].bitcast(I32), os_t[32 * q : 32 * q + 4, :].bitcast(I32))

@@ -29,8 +29,8 @@ def tile_picked_skipputbhop_none_po_kernel(tc, x_words, x_scales, w1_words, w1_s
         keep = ctx.enter_context(tc.tile_pool(name="keep", bufs=1))
         psum = ctx.enter_context(tc.psum_pool(name="psum", bufs=1))
 
-        def sb(name, shape, dtype):
-            return keep.tile(shape, dtype, name=name, align_bytes=64)
+        def sb(name, shape, dtype, tag=None):
+            return keep.tile(shape, dtype, name=name, tag=tag or name, align_bytes=64)
 
         def load_list(name, src):
             tile = keep.tile(list(src.shape), U16, name=name)
@@ -40,36 +40,37 @@ def tile_picked_skipputbhop_none_po_kernel(tc, x_words, x_scales, w1_words, w1_s
         def cols16(lst, start, count):
             return lst[:, start // 16 : (start + count) // 16]
 
-        def load_scales(queue, tile, src):
+        def load_scales(queues, tile, src, first):
             for q in range(4):
-                queue.dma_start(tile[32 * q : 32 * q + 4, :].bitcast(I32), src[0, 4 * q : 4 * q + 4, :].bitcast(I32))
+                queues[q].dma_start(tile[32 * q + first : 32 * q + first + 4, :].bitcast(I32), src[0, 4 * q : 4 * q + 4, :].bitcast(I32))
 
         def load_words(tile, src):
             nc.sync.dma_start(tile[:], src[0].rearrange("p c r -> p (c r)").bitcast(I32))
 
         xs = sb("xs", [P, T], U8)
-        w1s_raw = sb("w1s_raw", [P, H], U8)
+        ws_raw = sb("ws_raw", [P, H], U8)
         w2s_raw = sb("w2s_raw", [P, N], U8)
         warm = sb("warm", [P, 2], F32)
-        nc.vector.memset(xs[:].bitcast(I32), 0)
-        nc.vector.memset(w1s_raw[:].bitcast(I32), 0)
-        nc.vector.memset(w2s_raw[:].bitcast(I32), 0)
+        nc.vector.memset(xs[:, : T // 2].bitcast(I32), 0)
+        nc.gpsimd.memset(xs[:, T // 2 :].bitcast(I32), 0)
+        nc.vector.memset(ws_raw[:].bitcast(I32), 0)
+        nc.gpsimd.memset(w2s_raw[:].bitcast(I32), 0)
         nc.vector.memset(warm[:, 0:1], 0.0)
 
-        load_scales(nc.scalar, xs, x_scales)
+        load_scales([nc.sync, nc.scalar] * 2, xs, x_scales, 0)
         nc.scalar.activation(warm[:, 1:2], warm[:, 0:1], COPY, scale=-1.0)
-        xw = sb("xw", [P, T], I32)
-        load_words(xw, x_words)
         offs_t = load_list("offs_t", offs)
         w1w_raw = sb("w1w_raw", [P, H], I32)
         load_words(w1w_raw, w1_words)
-        load_scales(nc.sync, w1s_raw, w1_scales)
         gain = sb("gain", [P, PACK], F32)
         nc.sync.dma_start(gain[:], gn.rearrange("(p t) o -> p (t o)", t=PACK))
+        xw = sb("xw", [P, T], I32)
+        load_words(xw, x_words)
+        load_scales([nc.sync] * 4, ws_raw, w1_scales, 0)
         n1_t = load_list("n1_t", n1)
         w2w_raw = sb("w2w_raw", [P, N], I32)
         load_words(w2w_raw, w2_words)
-        load_scales(nc.sync, w2s_raw, w2_scales)
+        load_scales([nc.sync] * 4, w2s_raw, w2_scales, 0)
         n2_t = load_list("n2_t", n2)
         n4_t = load_list("n4_t", n4)
         n3_t = load_list("n3_t", n3)
@@ -82,43 +83,45 @@ def tile_picked_skipputbhop_none_po_kernel(tc, x_words, x_scales, w1_words, w1_s
         xg_s = sb("xg_s", [P, S], U8)
         nc.vector.tensor_copy(xg_s[:], xs[:].indirect(offs_t[:]))
         w1w = deal("w1w", w1w_raw, I32)
-        w1s = deal("w1s", w1s_raw, U8)
+        w1s = deal("w1s", ws_raw, U8)
 
         neg_gain = sb("neg_gain", [P, PACK], F32)
         neg_half = sb("neg_half", [P, PACK], F32)
         nc.scalar.activation(neg_gain[:], gain[:], COPY, scale=-1.0)
         nc.scalar.activation(neg_half[:], gain[:], COPY, scale=-0.5)
 
-        y_ps = {}
+        halves = [slice(c * HALF, (c + 1) * HALF) for c in range(2)]
+        first = [psum.tile([P, HALF], F32, name="y_first%d" % c) for c in range(2)]
+        rest = [psum.tile([P, S], F32, name="y_rest%d" % t) for t in range(1, PACK)]
+        y_parts = [[(halves[c], first[c][:]) for c in range(2)]] + [[(slice(0, S), bank[:])] for bank in rest]
+        xg_w = [sb("xg_w%d" % c, [P, HALF], U32) for c in range(2)]
         for c in range(2):
-            xg_w = sb("xg_w%d" % c, [P, HALF], U32)
-            nc.vector.tensor_copy(xg_w[:], xw[:].bitcast(U32).indirect(cols16(offs_t, c * HALF, HALF)))
-            for u in range(2):
-                bank = psum.tile([P, 2, HALF], F32, name="y_ps%d%d" % (c, u))
-                for e in range(2):
-                    t = 2 * u + e
-                    nc.tensor.matmul_mx(
-                        out=bank[:, e, :],
-                        lhsT=w1w[:, t, :].bitcast(FP8X4),
-                        lhsT_scale=w1s[:, t, :],
-                        rhs=xg_w[:].bitcast(FP8X4),
-                        rhs_scale=xg_s[:, c * HALF : (c + 1) * HALF],
-                        start=True,
-                        stop=True,
-                    )
-                    y_ps[c, t] = bank[:, e, :]
+            nc.vector.tensor_copy(xg_w[c][:], xw[:].bitcast(U32).indirect(cols16(offs_t, c * HALF, HALF)))
+        for t in range(PACK):
+            for c in range(2):
+                nc.tensor.matmul_mx(
+                    out=first[c][:] if t == 0 else rest[t - 1][:, halves[c]],
+                    lhsT=w1w[:, t, :].bitcast(FP8X4),
+                    lhsT_scale=w1s[:, t, :],
+                    rhs=xg_w[c][:].bitcast(FP8X4),
+                    rhs_scale=xg_s[:, halves[c]],
+                    start=True,
+                    stop=True,
+                )
 
         w2w = deal("w2w", w2w_raw, I32)
         w2s = deal("w2s", w2s_raw, U8)
 
-        halves = [slice(c * HALF, (c + 1) * HALF) for c in range(2)]
         st = []
         for t in range(PACK):
             y_half = sb("y_half%d" % t, [P, S], F32)
             y_full = sb("y_full%d" % t, [P, S], F32)
-            for c in range(2):
-                nc.scalar.activation(y_half[:, halves[c]], y_ps[c, t], COPY, scale=neg_half[:, t : t + 1])
-                nc.scalar.activation(y_full[:, halves[c]], y_ps[c, t], COPY, scale=neg_gain[:, t : t + 1])
+            for cols, part in y_parts[t]:
+                if cols.start == HALF:
+                    nc.vector.tensor_scalar(y_half[:, cols], part, neg_half[:, t : t + 1], None, MULT)
+                else:
+                    nc.scalar.activation(y_half[:, cols], part, COPY, scale=neg_half[:, t : t + 1])
+                nc.scalar.activation(y_full[:, cols], part, COPY, scale=neg_gain[:, t : t + 1])
             s_t = sb("st%d" % t, [P, S], F32)
             for c in range(2):
                 nc.vector.tensor_tensor(s_t[:, halves[c]], y_half[:].indirect(cols16(n1_t, c * HALF, HALF)), y_full[:, halves[c]], ADD)
@@ -136,14 +139,14 @@ def tile_picked_skipputbhop_none_po_kernel(tc, x_words, x_scales, w1_words, w1_s
         y_raw = []
         for t in range(PACK):
             y_t = sb("y_raw%d" % t, [P, S], F32)
-            for c in range(2):
-                nc.scalar.copy(y_t[:, halves[c]], y_ps[c, t])
+            for cols, part in y_parts[t]:
+                nc.scalar.copy(y_t[:, cols], part)
             y_raw.append(y_t)
 
         h = [sb("h%d" % t, [P, S], F32) for t in range(PACK)]
         for start, width in Z_CHUNKS:
             cols = slice(start, start + width)
-            z = sb("z%d" % start, [P, PACK, width], F32)
+            z = sb("z%d" % start, [P, PACK, width], F32, tag="zb0" if start == 384 else None)
             for t in range(PACK):
                 nc.vector.tensor_tensor(z[:, t, :], st[t][:].indirect(cols16(n2_t, start, width)), st_copy[t][:, cols], SUB)
             zb = sb("zb%d" % start, [P, width, PACK], BF16)
@@ -153,7 +156,7 @@ def tile_picked_skipputbhop_none_po_kernel(tc, x_words, x_scales, w1_words, w1_s
             nc.vector.quantize_mx(out=zw[:].bitcast(FP8X4), scales=zs[:], in_=zb[:].rearrange("p c t -> p (c t)"))
             per_bank = S // width
             for u in range(PACK // per_bank):
-                bank = psum.tile([P, per_bank, width], F32, name="h_ps%d_%d" % (start, u))
+                bank = psum.tile([P, per_bank, width], F32, name="h_ps%d_%d" % (start, u), tag="y_first0" if start == 384 else "h_ps%d_%d" % (start, u))
                 for e in range(per_bank):
                     t = per_bank * u + e
                     nc.tensor.matmul_mx(
@@ -168,18 +171,17 @@ def tile_picked_skipputbhop_none_po_kernel(tc, x_words, x_scales, w1_words, w1_s
                 for e in range(per_bank):
                     nc.scalar.copy(h[per_bank * u + e][:, cols], bank[:, e, :])
 
-        y_n4 = []
+        after_quant = sb("y_n4_late", [P, 2, W], F32, tag="zb384")
+        y_n4 = [st_copy[0][:, HALF:], st_copy[1][:, HALF:], after_quant[:, 0, :], after_quant[:, 1, :]]
         for t in range(PACK):
-            g = sb("y_n4_%d" % t, [P, W], F32)
-            nc.vector.tensor_copy(g[:], y_raw[t][:].indirect(n4_t[:]))
-            y_n4.append(g)
+            nc.vector.tensor_copy(y_n4[t], y_raw[t][:].indirect(n4_t[:]))
 
         out_rows = out_0.rearrange("(p t) j -> t p j", t=PACK)
         ob = [sb("ob%d" % c, [P, HALF, PACK], BF16) for c in range(2)]
         for t in range(PACK):
             g = sb("h_n3_%d" % t, [P, W], F32)
             nc.vector.tensor_scalar(g[:], h[t][:].indirect(n3_t[:]), -0.5, 0.0, MULT, ADD)
-            nc.vector.tensor_tensor(h[t][:].indirect(n3_t[:]), y_n4[t][:], g[:], ADD)
+            nc.vector.tensor_tensor(h[t][:].indirect(n3_t[:]), y_n4[t], g[:], ADD)
             nc.sync.dma_start(out_rows[t], h[t][:])
             if t < 2:
                 nc.scalar.copy(ob[0][:, :, t], h[t][:, halves[0]])

@@ -66,7 +66,7 @@ def tile_picked_skipputbhop_none_po_kernel(tc, x_words, x_scales, w1_words, w1_s
         nc.sync.dma_start(gain[:], gn.rearrange("(p t) o -> p (t o)", t=PACK))
         xw = sb("xw", [P, T], I32)
         load_words(xw, x_words)
-        load_scales([nc.sync] * 4, ws_raw, w1_scales, 0)
+        load_scales([nc.scalar] * 4, ws_raw, w1_scales, 0)
         n1_t = load_list("n1_t", n1)
         w2w_raw = sb("w2w_raw", [P, N], I32)
         load_words(w2w_raw, w2_words)
@@ -94,7 +94,7 @@ def tile_picked_skipputbhop_none_po_kernel(tc, x_words, x_scales, w1_words, w1_s
         first = [psum.tile([P, HALF], F32, name="y_first%d" % c) for c in range(2)]
         rest = [psum.tile([P, S], F32, name="y_rest%d" % t) for t in range(1, PACK)]
         y_parts = [[(halves[c], first[c][:]) for c in range(2)]] + [[(slice(0, S), bank[:])] for bank in rest]
-        xg_w = [sb("xg_w%d" % c, [P, HALF], U32) for c in range(2)]
+        xg_w = [sb("xg_w0", [P, HALF], U32), sb("xg_w1", [P, HALF], U32, tag="ws_raw")]
         for c in range(2):
             nc.vector.tensor_copy(xg_w[c][:], xw[:].bitcast(U32).indirect(cols16(offs_t, c * HALF, HALF)))
         for t in range(PACK):
@@ -130,10 +130,8 @@ def tile_picked_skipputbhop_none_po_kernel(tc, x_words, x_scales, w1_words, w1_s
         st_copy = []
         for t in range(PACK):
             cp = sb("st_copy%d" % t, [P, S], F32)
-            if t < 2:
-                nc.sync.dma_start(cp[:], st[t][:])
-            else:
-                nc.scalar.copy(cp[:], st[t][:])
+            for cols in halves:
+                nc.sync.dma_start(cp[:, cols], st[t][:, cols])
             st_copy.append(cp)
 
         y_raw = []

@@ -75,15 +75,18 @@ def tile_picked_skipputbhop_none_po_kernel(tc, x_words, x_scales, w1_words, w1_s
         n4_t = load_list("n4_t", n4)
         n3_t = load_list("n3_t", n3)
 
-        def deal(name, raw, dtype):
-            tile = sb(name, [P, PACK, P], dtype)
-            nc.vector.tensor_copy(tile[:], raw[:].rearrange("p (m t) -> p t m", t=PACK))
+        def deal(name, raw, dtype, run, tag=None):
+            tile = sb(name, [P, PACK, P], dtype, tag=tag)
+            nc.vector.tensor_copy(
+                tile[:].rearrange("p t (c i) -> p c t i", i=run),
+                raw[:].rearrange("p (c i t) -> p c t i", i=run, t=PACK),
+            )
             return tile
 
         xg_s = sb("xg_s", [P, S], U8)
         nc.vector.tensor_copy(xg_s[:], xs[:].indirect(offs_t[:]))
-        w1w = deal("w1w", w1w_raw, I32)
-        w1s = deal("w1s", ws_raw, U8)
+        w1w = deal("w1w", w1w_raw, I32, 4)
+        w1s = deal("w1s", ws_raw, U8, 16)
 
         neg_gain = sb("neg_gain", [P, PACK], F32)
         neg_half = sb("neg_half", [P, PACK], F32)
@@ -109,8 +112,8 @@ def tile_picked_skipputbhop_none_po_kernel(tc, x_words, x_scales, w1_words, w1_s
                     stop=True,
                 )
 
-        w2w = deal("w2w", w2w_raw, I32)
-        w2s = deal("w2s", w2s_raw, U8)
+        w2w = deal("w2w", w2w_raw, I32, 4)
+        w2s = deal("w2s", w2s_raw, U8, 16)
 
         st = []
         for t in range(PACK):
@@ -129,10 +132,10 @@ def tile_picked_skipputbhop_none_po_kernel(tc, x_words, x_scales, w1_words, w1_s
 
         st_copy = []
         for t in range(PACK):
-            cp = sb("st_copy%d" % t, [P, S], F32)
-            for cols in halves:
-                nc.sync.dma_start(cp[:, cols], st[t][:, cols])
-            st_copy.append(cp)
+            parts = [sb("st_copy%d_%d" % (t, c), [P, HALF], F32) for c in range(2)]
+            for c in range(2):
+                nc.sync.dma_start(parts[c][:], st[t][:, halves[c]])
+            st_copy.append(parts)
 
         y_raw = []
         for t in range(PACK):
@@ -144,9 +147,9 @@ def tile_picked_skipputbhop_none_po_kernel(tc, x_words, x_scales, w1_words, w1_s
         h = [sb("h%d" % t, [P, S], F32) for t in range(PACK)]
         for start, width in Z_CHUNKS:
             cols = slice(start, start + width)
-            z = sb("z%d" % start, [P, PACK, width], F32, tag="zb0" if start == 384 else None)
+            z = sb("z%d" % start, [P, PACK, width], F32, tag={0: None, 256: "st_copy3_0", 384: "zb0"}[start])
             for t in range(PACK):
-                nc.vector.tensor_tensor(z[:, t, :], st[t][:].indirect(cols16(n2_t, start, width)), st_copy[t][:, cols], SUB)
+                nc.vector.tensor_tensor(z[:, t, :], st[t][:].indirect(cols16(n2_t, start, width)), st_copy[t][start // HALF][:, start % HALF : start % HALF + width], SUB)
             zb = sb("zb%d" % start, [P, width, PACK], BF16)
             nc.scalar.copy(zb[:].rearrange("p (c i) t -> p c t i", i=4), z[:].rearrange("p t (c i) -> p c t i", i=4))
             zw = sb("zw%d" % start, [P, width], U32)
@@ -170,7 +173,7 @@ def tile_picked_skipputbhop_none_po_kernel(tc, x_words, x_scales, w1_words, w1_s
                     nc.scalar.copy(h[per_bank * u + e][:, cols], bank[:, e, :])
 
         after_quant = sb("y_n4_late", [P, 2, W], F32, tag="zb384")
-        y_n4 = [st_copy[0][:, HALF:], st_copy[1][:, HALF:], after_quant[:, 0, :], after_quant[:, 1, :]]
+        y_n4 = [st_copy[0][1][:], st_copy[1][1][:], after_quant[:, 0, :], after_quant[:, 1, :]]
         for t in range(PACK):
             nc.vector.tensor_copy(y_n4[t], y_raw[t][:].indirect(n4_t[:]))
 
@@ -183,9 +186,9 @@ def tile_picked_skipputbhop_none_po_kernel(tc, x_words, x_scales, w1_words, w1_s
             nc.sync.dma_start(out_rows[t], h[t][:])
             if t < 2:
                 nc.scalar.copy(ob[0][:, :, t], h[t][:, halves[0]])
-            else:
-                nc.vector.tensor_copy(ob[0][:, :, t], h[t][:, halves[0]])
             nc.scalar.copy(ob[1][:, :, t], h[t][:, halves[1]])
+        for t in range(2, PACK):
+            nc.vector.tensor_copy(ob[0][:, :, t], h[t][:, halves[0]])
 
         os_t = sb("os_t", [P, S], U8)
         words_out = out_1[0].rearrange("p c r -> p (c r)").bitcast(I32)

@@ -19,11 +19,16 @@ COPY = mybir.ActivationFunctionType.Copy
 
 P = 128
 PACK = 4
+QUADRANTS = 4
+LINE = 16
 HALF = S // 2
+HALVES = (slice(0, HALF), slice(HALF, S))
 Z_CHUNKS = ((0, 256), (256, 128), (384, 128))
 
 
-def tile_picked_skipputbhop_none_po_kernel(tc, x_words, x_scales, w1_words, w1_scales, gn, w2_words, w2_scales, offs, n1, n2, n3, n4, out_0, out_1, out_2):
+def tile_picked_skipputbhop_none_po_kernel(
+    tc, x_words, x_scales, w1_words, w1_scales, gn, w2_words, w2_scales, offs, n1, n2, n3, n4, out_0, out_1, out_2
+):
     nc = tc.nc
     with ExitStack() as ctx:
         keep = ctx.enter_context(tc.tile_pool(name="keep", bufs=1))
@@ -37,28 +42,48 @@ def tile_picked_skipputbhop_none_po_kernel(tc, x_words, x_scales, w1_words, w1_s
             nc.sync.dma_start(tile[:], src)
             return tile
 
-        def cols16(lst, start, count):
+        def entries(lst, start, count):
             return lst[:, start // 16 : (start + count) // 16]
 
-        def load_scales(queues, tile, src, first):
-            for q in range(4):
-                queues[q].dma_start(tile[32 * q + first : 32 * q + first + 4, :].bitcast(I32), src[0, 4 * q : 4 * q + 4, :].bitcast(I32))
+        def load_scales(queues, tile, src):
+            for q in range(QUADRANTS):
+                queues[q].dma_start(tile[32 * q : 32 * q + 4, :].bitcast(I32), src[0, 4 * q : 4 * q + 4, :].bitcast(I32))
 
         def load_words(tile, src):
             nc.sync.dma_start(tile[:], src[0].rearrange("p c r -> p (c r)").bitcast(I32))
 
+        def deal(name, raw, dtype, size):
+            run = LINE // size
+            tile = sb(name, [P, PACK, P], dtype)
+            nc.vector.tensor_copy(
+                tile[:].rearrange("p t (c i) -> p c t i", i=run),
+                raw[:].rearrange("p (c i t) -> p c t i", i=run, t=PACK),
+            )
+            return tile
+
+        def multiply(out, words, scales, t, rhs_words, rhs_scales):
+            nc.tensor.matmul_mx(
+                out=out,
+                lhsT=words[:, t, :].bitcast(FP8X4),
+                lhsT_scale=scales[:, t, :],
+                rhs=rhs_words.bitcast(FP8X4),
+                rhs_scale=rhs_scales,
+                start=True,
+                stop=True,
+            )
+
         xs = sb("xs", [P, T], U8)
-        ws_raw = sb("ws_raw", [P, H], U8)
+        w1s_raw = sb("w1s_raw", [P, H], U8)
         w2s_raw = sb("w2s_raw", [P, N], U8)
-        warm = sb("warm", [P, 2], F32)
+        half = sb("half", [P, 2], F32)
         nc.vector.memset(xs[:, : T // 2].bitcast(I32), 0)
         nc.gpsimd.memset(xs[:, T // 2 :].bitcast(I32), 0)
-        nc.vector.memset(ws_raw[:].bitcast(I32), 0)
+        nc.vector.memset(w1s_raw[:].bitcast(I32), 0)
         nc.gpsimd.memset(w2s_raw[:].bitcast(I32), 0)
-        nc.vector.memset(warm[:, 0:1], 0.0)
+        nc.vector.memset(half[:, 0:1], 0.5)
 
-        load_scales([nc.sync, nc.scalar] * 2, xs, x_scales, 0)
-        nc.scalar.activation(warm[:, 1:2], warm[:, 0:1], COPY, scale=-1.0)
+        load_scales([nc.sync, nc.scalar] * 2, xs, x_scales)
+        nc.scalar.activation(half[:, 1:2], half[:, 0:1], COPY, scale=-1.0)
         offs_t = load_list("offs_t", offs)
         w1w_raw = sb("w1w_raw", [P, H], I32)
         load_words(w1w_raw, w1_words)
@@ -66,136 +91,124 @@ def tile_picked_skipputbhop_none_po_kernel(tc, x_words, x_scales, w1_words, w1_s
         nc.sync.dma_start(gain[:], gn.rearrange("(p t) o -> p (t o)", t=PACK))
         xw = sb("xw", [P, T], I32)
         load_words(xw, x_words)
-        load_scales([nc.scalar] * 4, ws_raw, w1_scales, 0)
+        load_scales([nc.scalar] * QUADRANTS, w1s_raw, w1_scales)
         n1_t = load_list("n1_t", n1)
         w2w_raw = sb("w2w_raw", [P, N], I32)
         load_words(w2w_raw, w2_words)
-        load_scales([nc.sync] * 4, w2s_raw, w2_scales, 0)
+        load_scales([nc.sync] * QUADRANTS, w2s_raw, w2_scales)
         n2_t = load_list("n2_t", n2)
         n4_t = load_list("n4_t", n4)
         n3_t = load_list("n3_t", n3)
 
-        def deal(name, raw, dtype, run, tag=None):
-            tile = sb(name, [P, PACK, P], dtype, tag=tag)
-            nc.vector.tensor_copy(
-                tile[:].rearrange("p t (c i) -> p c t i", i=run),
-                raw[:].rearrange("p (c i t) -> p c t i", i=run, t=PACK),
-            )
-            return tile
-
         xg_s = sb("xg_s", [P, S], U8)
         nc.vector.tensor_copy(xg_s[:], xs[:].indirect(offs_t[:]))
         w1w = deal("w1w", w1w_raw, I32, 4)
-        w1s = deal("w1s", ws_raw, U8, 16)
+        w1s = deal("w1s", w1s_raw, U8, 1)
 
         neg_gain = sb("neg_gain", [P, PACK], F32)
         neg_half = sb("neg_half", [P, PACK], F32)
         nc.scalar.activation(neg_gain[:], gain[:], COPY, scale=-1.0)
-        nc.scalar.activation(neg_half[:], gain[:], COPY, scale=-0.5)
+        nc.scalar.activation(neg_half[:], gain[:], COPY, scale=half[:, 1:2])
 
-        halves = [slice(c * HALF, (c + 1) * HALF) for c in range(2)]
-        first = [psum.tile([P, HALF], F32, name="y_first%d" % c) for c in range(2)]
-        rest = [psum.tile([P, S], F32, name="y_rest%d" % t) for t in range(1, PACK)]
-        y_parts = [[(halves[c], first[c][:]) for c in range(2)]] + [[(slice(0, S), bank[:])] for bank in rest]
-        xg_w = [sb("xg_w0", [P, HALF], U32), sb("xg_w1", [P, HALF], U32, tag="ws_raw")]
+        y_first = [psum.tile([P, HALF], F32, name="y_first%d" % c) for c in range(2)]
+        y_rest = [psum.tile([P, S], F32, name="y_rest%d" % t) for t in range(1, PACK)]
+        y_parts = [[(HALVES[c], y_first[c][:]) for c in range(2)]] + [[(slice(0, S), bank[:])] for bank in y_rest]
+        xg_w = [sb("xg_w0", [P, HALF], U32), sb("xg_w1", [P, HALF], U32, tag="w1s_raw")]
         for c in range(2):
-            nc.vector.tensor_copy(xg_w[c][:], xw[:].bitcast(U32).indirect(cols16(offs_t, c * HALF, HALF)))
+            nc.vector.tensor_copy(xg_w[c][:], xw[:].bitcast(U32).indirect(entries(offs_t, c * HALF, HALF)))
         for t in range(PACK):
             for c in range(2):
-                nc.tensor.matmul_mx(
-                    out=first[c][:] if t == 0 else rest[t - 1][:, halves[c]],
-                    lhsT=w1w[:, t, :].bitcast(FP8X4),
-                    lhsT_scale=w1s[:, t, :],
-                    rhs=xg_w[c][:].bitcast(FP8X4),
-                    rhs_scale=xg_s[:, halves[c]],
-                    start=True,
-                    stop=True,
-                )
+                bank = y_first[c][:] if t == 0 else y_rest[t - 1][:, HALVES[c]]
+                multiply(bank, w1w, w1s, t, xg_w[c][:], xg_s[:, HALVES[c]])
 
         w2w = deal("w2w", w2w_raw, I32, 4)
-        w2s = deal("w2s", w2s_raw, U8, 16)
+        w2s = deal("w2s", w2s_raw, U8, 1)
 
-        st = []
+        s = []
         for t in range(PACK):
             y_half = sb("y_half%d" % t, [P, S], F32)
             y_full = sb("y_full%d" % t, [P, S], F32)
             for cols, part in y_parts[t]:
-                if cols.start == HALF:
+                if cols == HALVES[1]:
                     nc.vector.tensor_scalar(y_half[:, cols], part, neg_half[:, t : t + 1], None, MULT)
                 else:
                     nc.scalar.activation(y_half[:, cols], part, COPY, scale=neg_half[:, t : t + 1])
                 nc.scalar.activation(y_full[:, cols], part, COPY, scale=neg_gain[:, t : t + 1])
-            s_t = sb("st%d" % t, [P, S], F32)
+            s_t = sb("s%d" % t, [P, S], F32)
             for c in range(2):
-                nc.vector.tensor_tensor(s_t[:, halves[c]], y_half[:].indirect(cols16(n1_t, c * HALF, HALF)), y_full[:, halves[c]], ADD)
-            st.append(s_t)
+                looked_up = y_half[:].indirect(entries(n1_t, c * HALF, HALF))
+                nc.vector.tensor_tensor(s_t[:, HALVES[c]], looked_up, y_full[:, HALVES[c]], ADD)
+            s.append(s_t)
 
-        st_copy = []
+        s_copy = []
         for t in range(PACK):
-            parts = [sb("st_copy%d_%d" % (t, c), [P, HALF], F32) for c in range(2)]
+            parts = [sb("s_copy%d_%d" % (t, c), [P, HALF], F32) for c in range(2)]
             for c in range(2):
-                nc.sync.dma_start(parts[c][:], st[t][:, halves[c]])
-            st_copy.append(parts)
+                nc.sync.dma_start(parts[c][:], s[t][:, HALVES[c]])
+            s_copy.append(parts)
 
-        y_raw = []
+        y = []
         for t in range(PACK):
-            y_t = sb("y_raw%d" % t, [P, S], F32)
+            y_t = sb("y%d" % t, [P, S], F32)
             for cols, part in y_parts[t]:
                 nc.scalar.copy(y_t[:, cols], part)
-            y_raw.append(y_t)
+            y.append(y_t)
 
+        z_tags = (None, "s_copy3_0", "zb0")
         h = [sb("h%d" % t, [P, S], F32) for t in range(PACK)]
-        for start, width in Z_CHUNKS:
+        h_parts = [[] for t in range(PACK)]
+        for j, (start, width) in enumerate(Z_CHUNKS):
             cols = slice(start, start + width)
-            z = sb("z%d" % start, [P, PACK, width], F32, tag={0: None, 256: "st_copy3_0", 384: "zb0"}[start])
+            z = sb("z%d" % j, [P, PACK, width], F32, tag=z_tags[j])
             for t in range(PACK):
-                nc.vector.tensor_tensor(z[:, t, :], st[t][:].indirect(cols16(n2_t, start, width)), st_copy[t][start // HALF][:, start % HALF : start % HALF + width], SUB)
-            zb = sb("zb%d" % start, [P, width, PACK], BF16)
+                plain = s_copy[t][start // HALF][:, start % HALF : start % HALF + width]
+                nc.vector.tensor_tensor(z[:, t, :], s[t][:].indirect(entries(n2_t, start, width)), plain, SUB)
+            zb = sb("zb%d" % j, [P, width, PACK], BF16)
             nc.scalar.copy(zb[:].rearrange("p (c i) t -> p c t i", i=4), z[:].rearrange("p t (c i) -> p c t i", i=4))
-            zw = sb("zw%d" % start, [P, width], U32)
-            zs = sb("zs%d" % start, [P, width], U8)
+            zw = sb("zw%d" % j, [P, width], U32)
+            zs = sb("zs%d" % j, [P, width], U8)
             nc.vector.quantize_mx(out=zw[:].bitcast(FP8X4), scales=zs[:], in_=zb[:].rearrange("p c t -> p (c t)"))
             per_bank = S // width
             for u in range(PACK // per_bank):
-                bank = psum.tile([P, per_bank, width], F32, name="h_ps%d_%d" % (start, u), tag="y_first0" if start == 384 else "h_ps%d_%d" % (start, u))
+                name = "h_ps%d_%d" % (j, u)
+                last = j == len(Z_CHUNKS) - 1
+                bank = psum.tile([P, per_bank, width], F32, name=name, tag="y_first0" if last else name)
                 for e in range(per_bank):
                     t = per_bank * u + e
-                    nc.tensor.matmul_mx(
-                        out=bank[:, e, :],
-                        lhsT=w2w[:, t, :].bitcast(FP8X4),
-                        lhsT_scale=w2s[:, t, :],
-                        rhs=zw[:].bitcast(FP8X4),
-                        rhs_scale=zs[:],
-                        start=True,
-                        stop=True,
-                    )
-                for e in range(per_bank):
-                    nc.scalar.copy(h[per_bank * u + e][:, cols], bank[:, e, :])
-
-        after_quant = sb("y_n4_late", [P, 2, W], F32, tag="zb384")
-        y_n4 = [st_copy[0][1][:], st_copy[1][1][:], after_quant[:, 0, :], after_quant[:, 1, :]]
+                    multiply(bank[:, e, :], w2w, w2s, t, zw[:], zs[:])
+                    h_parts[t].append((cols, bank[:, e, :]))
         for t in range(PACK):
-            nc.vector.tensor_copy(y_n4[t], y_raw[t][:].indirect(n4_t[:]))
+            for cols, part in h_parts[t]:
+                nc.scalar.copy(h[t][:, cols], part)
+
+        y_n4_late = sb("y_n4_late", [P, 2, W], F32, tag="zb2")
+        y_n4 = [s_copy[0][1][:], s_copy[1][1][:], y_n4_late[:, 0, :], y_n4_late[:, 1, :]]
+        for t in range(PACK):
+            nc.vector.tensor_copy(y_n4[t], y[t][:].indirect(n4_t[:]))
 
         out_rows = out_0.rearrange("(p t) j -> t p j", t=PACK)
         ob = [sb("ob%d" % c, [P, HALF, PACK], BF16) for c in range(2)]
         for t in range(PACK):
-            g = sb("h_n3_%d" % t, [P, W], F32)
-            nc.vector.tensor_scalar(g[:], h[t][:].indirect(n3_t[:]), -0.5, 0.0, MULT, ADD)
-            nc.vector.tensor_tensor(h[t][:].indirect(n3_t[:]), y_n4[t], g[:], ADD)
+            h_n3 = sb("h_n3_%d" % t, [P, W], F32)
+            nc.vector.tensor_scalar(h_n3[:], h[t][:].indirect(n3_t[:]), -0.5, 0.0, MULT, ADD)
+            nc.vector.tensor_tensor(h[t][:].indirect(n3_t[:]), y_n4[t], h_n3[:], ADD)
             nc.sync.dma_start(out_rows[t], h[t][:])
             if t < 2:
-                nc.scalar.copy(ob[0][:, :, t], h[t][:, halves[0]])
-            nc.scalar.copy(ob[1][:, :, t], h[t][:, halves[1]])
+                nc.scalar.copy(ob[0][:, :, t], h[t][:, HALVES[0]])
+            nc.scalar.copy(ob[1][:, :, t], h[t][:, HALVES[1]])
         for t in range(2, PACK):
-            nc.vector.tensor_copy(ob[0][:, :, t], h[t][:, halves[0]])
+            nc.vector.tensor_copy(ob[0][:, :, t], h[t][:, HALVES[0]])
 
-        os_t = sb("os_t", [P, S], U8)
+        out_scales = sb("out_scales", [P, S], U8)
         words_out = out_1[0].rearrange("p c r -> p (c r)").bitcast(I32)
         for c in range(2):
-            ow = sb("ow%d" % c, [P, HALF], U32)
-            nc.vector.quantize_mx(out=ow[:].bitcast(FP8X4), scales=os_t[:, halves[c]], in_=ob[c][:].rearrange("p c t -> p (c t)"))
-            nc.sync.dma_start(words_out[:, halves[c]], ow[:].bitcast(I32))
-        for q in range(4):
+            out_words = sb("out_words%d" % c, [P, HALF], U32)
+            nc.vector.quantize_mx(
+                out=out_words[:].bitcast(FP8X4),
+                scales=out_scales[:, HALVES[c]],
+                in_=ob[c][:].rearrange("p c t -> p (c t)"),
+            )
+            nc.sync.dma_start(words_out[:, HALVES[c]], out_words[:].bitcast(I32))
+        for q in range(QUADRANTS):
             queue = nc.sync if q % 2 == 0 else nc.scalar
-            queue.dma_start(out_2[0, 4 * q : 4 * q + 4, :].bitcast(I32), os_t[32 * q : 32 * q + 4, :].bitcast(I32))
+            queue.dma_start(out_2[0, 4 * q : 4 * q + 4, :].bitcast(I32), out_scales[32 * q : 32 * q + 4, :].bitcast(I32))

from contextlib import ExitStack

import concourse.mybir as mybir

K, T, S, N, H, W = 512, 2048, 512, 512, 512, 256
FLOPS = 2 * K * H * S + 2 * H * N * S

F32 = mybir.dt.float32
BF16 = mybir.dt.bfloat16
I32 = mybir.dt.int32
U32 = mybir.dt.uint32
U16 = mybir.dt.uint16
U8 = mybir.dt.uint8
FP8X4 = mybir.dt.float8_e4m3fn_x4
ADD = mybir.AluOpType.add
SUB = mybir.AluOpType.subtract
MULT = mybir.AluOpType.mult
COPY = mybir.ActivationFunctionType.Copy

P = 128
PACK = 4
QUADRANTS = 4
LINE = 16
HALF = S // 2
HALVES = (slice(0, HALF), slice(HALF, S))
Z_CHUNKS = ((0, 256), (256, 128), (384, 128))


def tile_picked_skipputbhop_none_po_kernel(
    tc, x_words, x_scales, w1_words, w1_scales, gn, w2_words, w2_scales, offs, n1, n2, n3, n4, out_0, out_1, out_2
):
    nc = tc.nc
    with ExitStack() as ctx:
        keep = ctx.enter_context(tc.tile_pool(name="keep", bufs=1))
        psum = ctx.enter_context(tc.psum_pool(name="psum", bufs=1))

        def sb(name, shape, dtype, tag=None):
            return keep.tile(shape, dtype, name=name, tag=tag or name, align_bytes=64)

        def load_list(name, src):
            tile = keep.tile(list(src.shape), U16, name=name)
            nc.sync.dma_start(tile[:], src)
            return tile

        def entries(lst, start, count):
            return lst[:, start // 16 : (start + count) // 16]

        def load_scales(queues, tile, src):
            for q in range(QUADRANTS):
                queues[q].dma_start(tile[32 * q : 32 * q + 4, :].bitcast(I32), src[0, 4 * q : 4 * q + 4, :].bitcast(I32))

        def load_words(tile, src):
            nc.sync.dma_start(tile[:], src[0].rearrange("p c r -> p (c r)").bitcast(I32))

        def deal(name, raw, dtype, size):
            run = LINE // size
            tile = sb(name, [P, PACK, P], dtype)
            nc.vector.tensor_copy(
                tile[:].rearrange("p t (c i) -> p c t i", i=run),
                raw[:].rearrange("p (c i t) -> p c t i", i=run, t=PACK),
            )
            return tile

        def multiply(out, words, scales, t, rhs_words, rhs_scales):
            nc.tensor.matmul_mx(
                out=out,
                lhsT=words[:, t, :].bitcast(FP8X4),
                lhsT_scale=scales[:, t, :],
                rhs=rhs_words.bitcast(FP8X4),
                rhs_scale=rhs_scales,
                start=True,
                stop=True,
            )

        xs = sb("xs", [P, T], U8)
        w1s_raw = sb("w1s_raw", [P, H], U8)
        w2s_raw = sb("w2s_raw", [P, N], U8)
        half = sb("half", [P, 2], F32)
        nc.vector.memset(xs[:, : T // 2].bitcast(I32), 0)
        nc.gpsimd.memset(xs[:, T // 2 :].bitcast(I32), 0)
        nc.vector.memset(w1s_raw[:].bitcast(I32), 0)
        nc.gpsimd.memset(w2s_raw[:].bitcast(I32), 0)
        nc.vector.memset(half[:, 0:1], 0.5)

        load_scales([nc.sync, nc.scalar] * 2, xs, x_scales)
        nc.scalar.activation(half[:, 1:2], half[:, 0:1], COPY, scale=-1.0)
        offs_t = load_list("offs_t", offs)
        w1w_raw = sb("w1w_raw", [P, H], I32)
        load_words(w1w_raw, w1_words)
        gain = sb("gain", [P, PACK], F32)
        nc.sync.dma_start(gain[:], gn.rearrange("(p t) o -> p (t o)", t=PACK))
        xw = sb("xw", [P, T], I32)
        load_words(xw, x_words)
        load_scales([nc.scalar] * QUADRANTS, w1s_raw, w1_scales)
        n1_t = load_list("n1_t", n1)
        w2w_raw = sb("w2w_raw", [P, N], I32)
        load_words(w2w_raw, w2_words)
        load_scales([nc.sync] * QUADRANTS, w2s_raw, w2_scales)
        n2_t = load_list("n2_t", n2)
        n4_t = load_list("n4_t", n4)
        n3_t = load_list("n3_t", n3)

        xg_s = sb("xg_s", [P, S], U8)
        nc.vector.tensor_copy(xg_s[:], xs[:].indirect(offs_t[:]))
        w1w = deal("w1w", w1w_raw, I32, 4)
        w1s = deal("w1s", w1s_raw, U8, 1)

        neg_gain = sb("neg_gain", [P, PACK], F32)
        neg_half = sb("neg_half", [P, PACK], F32)
        nc.scalar.activation(neg_gain[:], gain[:], COPY, scale=-1.0)
        nc.scalar.activation(neg_half[:], gain[:], COPY, scale=half[:, 1:2])

        y_first = [psum.tile([P, HALF], F32, name="y_first%d" % c) for c in range(2)]
        y_rest = [psum.tile([P, S], F32, name="y_rest%d" % t) for t in range(1, PACK)]
        y_parts = [[(HALVES[c], y_first[c][:]) for c in range(2)]] + [[(slice(0, S), bank[:])] for bank in y_rest]
        xg_w = [sb("xg_w0", [P, HALF], U32), sb("xg_w1", [P, HALF], U32, tag="w1s_raw")]
        for c in range(2):
            nc.vector.tensor_copy(xg_w[c][:], xw[:].bitcast(U32).indirect(entries(offs_t, c * HALF, HALF)))
        for t in range(PACK):
            for c in range(2):
                bank = y_first[c][:] if t == 0 else y_rest[t - 1][:, HALVES[c]]
                multiply(bank, w1w, w1s, t, xg_w[c][:], xg_s[:, HALVES[c]])

        w2w = deal("w2w", w2w_raw, I32, 4)
        w2s = deal("w2s", w2s_raw, U8, 1)

        s = []
        for t in range(PACK):
            y_half = sb("y_half%d" % t, [P, S], F32)
            y_full = sb("y_full%d" % t, [P, S], F32)
            for cols, part in y_parts[t]:
                if cols == HALVES[1]:
                    nc.vector.tensor_scalar(y_half[:, cols], part, neg_half[:, t : t + 1], None, MULT)
                else:
                    nc.scalar.activation(y_half[:, cols], part, COPY, scale=neg_half[:, t : t + 1])
                nc.scalar.activation(y_full[:, cols], part, COPY, scale=neg_gain[:, t : t + 1])
            s_t = sb("s%d" % t, [P, S], F32)
            for c in range(2):
                looked_up = y_half[:].indirect(entries(n1_t, c * HALF, HALF))
                nc.vector.tensor_tensor(s_t[:, HALVES[c]], looked_up, y_full[:, HALVES[c]], ADD)
            s.append(s_t)

        s_copy = []
        for t in range(PACK):
            parts = [sb("s_copy%d_%d" % (t, c), [P, HALF], F32) for c in range(2)]
            for c in range(2):
                nc.sync.dma_start(parts[c][:], s[t][:, HALVES[c]])
            s_copy.append(parts)

        y = []
        for t in range(PACK):
            y_t = sb("y%d" % t, [P, S], F32)
            for cols, part in y_parts[t]:
                nc.scalar.copy(y_t[:, cols], part)
            y.append(y_t)

        z_tags = (None, "s_copy3_0", "zb0")
        h = [sb("h%d" % t, [P, S], F32) for t in range(PACK)]
        h_parts = [[] for t in range(PACK)]
        for j, (start, width) in enumerate(Z_CHUNKS):
            cols = slice(start, start + width)
            z = sb("z%d" % j, [P, PACK, width], F32, tag=z_tags[j])
            for t in range(PACK):
                plain = s_copy[t][start // HALF][:, start % HALF : start % HALF + width]
                nc.vector.tensor_tensor(z[:, t, :], s[t][:].indirect(entries(n2_t, start, width)), plain, SUB)
            zb = sb("zb%d" % j, [P, width, PACK], BF16)
            nc.scalar.copy(zb[:].rearrange("p (c i) t -> p c t i", i=4), z[:].rearrange("p t (c i) -> p c t i", i=4))
            zw = sb("zw%d" % j, [P, width], U32)
            zs = sb("zs%d" % j, [P, width], U8)
            nc.vector.quantize_mx(out=zw[:].bitcast(FP8X4), scales=zs[:], in_=zb[:].rearrange("p c t -> p (c t)"))
            per_bank = S // width
            for u in range(PACK // per_bank):
                name = "h_ps%d_%d" % (j, u)
                last = j == len(Z_CHUNKS) - 1
                bank = psum.tile([P, per_bank, width], F32, name=name, tag="y_first0" if last else name)
                for e in range(per_bank):
                    t = per_bank * u + e
                    multiply(bank[:, e, :], w2w, w2s, t, zw[:], zs[:])
                    h_parts[t].append((cols, bank[:, e, :]))
        for t in range(PACK):
            for cols, part in h_parts[t]:
                nc.scalar.copy(h[t][:, cols], part)

        y_n4_late = sb("y_n4_late", [P, 2, W], F32, tag="zb2")
        y_n4 = [s_copy[0][1][:], s_copy[1][1][:], y_n4_late[:, 0, :], y_n4_late[:, 1, :]]
        for t in range(PACK):
            nc.vector.tensor_copy(y_n4[t], y[t][:].indirect(n4_t[:]))

        out_rows = out_0.rearrange("(p t) j -> t p j", t=PACK)
        ob = [sb("ob%d" % c, [P, HALF, PACK], BF16) for c in range(2)]
        for t in range(PACK):
            h_n3 = sb("h_n3_%d" % t, [P, W], F32)
            nc.vector.tensor_scalar(h_n3[:], h[t][:].indirect(n3_t[:]), -0.5, 0.0, MULT, ADD)
            nc.vector.tensor_tensor(h[t][:].indirect(n3_t[:]), y_n4[t], h_n3[:], ADD)
            nc.sync.dma_start(out_rows[t], h[t][:])
            if t < 2:
                nc.scalar.copy(ob[0][:, :, t], h[t][:, HALVES[0]])
            nc.scalar.copy(ob[1][:, :, t], h[t][:, HALVES[1]])
        for t in range(2, PACK):
            nc.vector.tensor_copy(ob[0][:, :, t], h[t][:, HALVES[0]])

        out_scales = sb("out_scales", [P, S], U8)
        words_out = out_1[0].rearrange("p c r -> p (c r)").bitcast(I32)
        for c in range(2):
            out_words = sb("out_words%d" % c, [P, HALF], U32)
            nc.vector.quantize_mx(
                out=out_words[:].bitcast(FP8X4),
                scales=out_scales[:, HALVES[c]],
                in_=ob[c][:].rearrange("p c t -> p (c t)"),
            )
            nc.sync.dma_start(words_out[:, HALVES[c]], out_words[:].bitcast(I32))
        for q in range(QUADRANTS):
            queue = nc.sync if q % 2 == 0 else nc.scalar
            queue.dma_start(out_2[0, 4 * q : 4 * q + 4, :].bitcast(I32), out_scales[32 * q : 32 * q + 4, :].bitcast(I32))
